import numpy as np
import ml_dtypes


def mxq(x, axis, fmt="e4m3"):
    dtype, down = {"e4m3": (ml_dtypes.float8_e4m3fn, 7), "e5m2": (ml_dtypes.float8_e5m2, 14)}[fmt]
    v = np.moveaxis(np.asarray(x, np.float32).astype(ml_dtypes.bfloat16).astype(np.float64), axis, -1)
    blocks = v.reshape(v.shape[:-1] + (-1, 32))
    amax = np.abs(blocks).max(-1, keepdims=True)
    byte = np.maximum(np.where(amax > 0, np.frexp(amax)[1] - 1 + 127, 0) - down, 1)
    scale = np.exp2(byte - 127.0)
    codes = (blocks / scale).astype(np.float32).astype(dtype).astype(np.float64)
    return np.moveaxis((codes * scale).reshape(v.shape), -1, axis)


WIDE = False


def mx_kscale(k):
    if not WIDE:
        return np.ones(k)
    levels = np.array([10, -10, 5, -5, 0])
    if k % 512:
        return np.exp2(np.random.permutation(np.resize(levels, k // 32))).repeat(32)
    a = np.empty((k // 512, 16))
    for p in range(k // 512):
        a[p, :8] = np.random.permutation(np.resize(levels, 8))
        for g in range(8):
            far = levels[np.abs(levels - a[p, g]) >= 10]
            a[p, g + 8] = far[np.random.randint(len(far))]
    return np.exp2(a.ravel()).repeat(32)


def f64(x):
    return np.asarray(x).astype(np.float64)


def striped(idx):
    return np.tile(idx.reshape(-1, 16).T, (8, 1)).astype(np.uint16)


def unstriped(offs):
    return offs[:16].T.reshape(-1).astype(np.int64)


E2M1 = np.array([0.0, 0.5, 1.0, 1.5, 2.0, 3.0, 4.0, 6.0, -0.0, -0.5, -1.0, -1.5, -2.0, -3.0, -4.0, -6.0])


def pack_weight(w, fmt):
    k, n = w.shape
    w = f64(np.asarray(w, np.float32).astype(ml_dtypes.bfloat16)).reshape(k // 32, 32, n)
    amax = np.abs(w).max(1)
    if fmt == "e4m3":
        byte = np.frexp(amax)[1] - 1 + 127 - 7
    else:
        mant, ex = np.frexp(amax / 6.0)
        byte = np.where(mant > 0.5, ex, ex - 1) + 127
    byte = np.clip(np.where(amax > 0, byte, 1), 1, 254)
    scaled = (w * np.exp2(127.0 - byte)[:, None, :]).reshape(k, n).astype(np.float32)
    by_word = np.ascontiguousarray(scaled.reshape(k // 512, 128, 4, n).transpose(0, 1, 3, 2))
    if fmt == "e4m3":
        words = by_word.astype(ml_dtypes.float8_e4m3fn).view(np.uint8)
    else:
        c = by_word.astype(ml_dtypes.float4_e2m1fn).view(np.uint8) & 0xF
        words = (c[..., 0::2] | (c[..., 1::2] << 4)).reshape(k // 512, 128, 2 * n)
    return np.ascontiguousarray(words), np.ascontiguousarray(byte.astype(np.uint8).reshape(k // 512, 16, n))


def unpack_weight(words, scales, fmt):
    g, _, n = scales.shape
    words = np.ascontiguousarray(words).reshape(g, 128, n, -1)
    if fmt == "e4m3":
        vals = words.view(ml_dtypes.float8_e4m3fn).astype(np.float64)
    else:
        nib = np.empty((g, 128, n, 4), np.uint8)
        nib[..., 0::2] = words & 0xF
        nib[..., 1::2] = words >> 4
        vals = E2M1[nib]
    vals = vals * np.repeat(np.exp2(scales.astype(np.float64) - 127.0), 8, axis=1)[..., None]
    return vals.transpose(0, 1, 3, 2).reshape(g * 512, n)


def gelu(v):
    return 0.5 * v * (1.0 + np.tanh(np.sqrt(2.0 / np.pi) * (v + 0.044715 * v**3)))


K, H, T, S, T2, P = 1024, 1024, 4096, 1024, 2048, 512

def setup_inputs():
    n = np.random.standard_normal
    s = mx_kscale(K)[:, None]
    u = mx_kscale(H)[:, None]
    tab_words, tab_scales = pack_weight(n((K, T)) * s, "e4m3")
    w4_words, w4_scales = pack_weight(0.36 * n((K, H)) / s / np.sqrt(K), "e2m1")
    return {
        "tab_words": tab_words, "tab_scales": tab_scales,
        "offs": striped(np.random.permutation(T)[:S]),
        "offs2": striped(np.random.permutation(T2)[:S]),
        "offs3": striped(np.random.permutation(T2)[:P]),
        "offs4": striped(np.random.permutation(T2)[:P]),
        "w4_words": w4_words, "w4_scales": w4_scales,
        "b1": np.random.uniform(-1.0, 1.0, H).astype(np.float32),
        "w2": (0.8 * n((K, H)) / s * u.T / np.sqrt(K)).astype(np.float32),
        "b2": (0.5 * n(H) * u[:, 0]).astype(np.float32),
        "page0": (n((H, T2)) * u).astype(np.float32),
        "wgs": np.exp(0.3 * n((128, S))).astype(np.float32),
        "zg": (n(H) / u[:, 0] ** 2 / np.sqrt(H)).astype(np.float32),
        "pairm": (0.6 * n((P, P))).astype(np.float32),
    }

def reference(tab_words, tab_scales, offs, offs2, offs3, offs4, w4_words, w4_scales, b1, w2, b2, page0, wgs, zg, pairm):
    v = unpack_weight(tab_words, tab_scales, "e4m3")[:, unstriped(offs)]
    w4 = unpack_weight(w4_words, w4_scales, "e2m1")
    ang = (w4.T @ v) + f64(b1)[:, None]
    val = (mxq(f64(w2), 0, "e4m3").T @ v) + f64(b2)[:, None]
    h = np.cos(ang) * val
    page = f64(page0).copy()
    page[:, unstriped(offs2)] = np.tile(f64(wgs), (H // 128, 1)) * h
    x1 = page[:, unstriped(offs3)]
    x2 = np.abs(page[:, unstriped(offs4)]) * f64(zg)[:, None]
    e = mxq(x1, 0, "e4m3").T @ mxq(x2, 0, "e4m3")
    return e + f64(pairm)

@@ -1,0 +1,401 @@
+import math
+from contextlib import ExitStack
+
+import concourse.mybir as mybir
+from concourse.masks import make_identity
+
+K, H, T, S, T2, PICKS = 1024, 1024, 4096, 1024, 2048, 512
+FLOPS = 2 * (2 * K * H * S + H * PICKS * PICKS)
+
+F32 = mybir.dt.float32
+BF16 = mybir.dt.bfloat16
+I32 = mybir.dt.int32
+U32 = mybir.dt.uint32
+U16 = mybir.dt.uint16
+U8 = mybir.dt.uint8
+FP8X4 = mybir.dt.float8_e4m3fn_x4
+FP4X4 = mybir.dt.float4_e2m1fn_x4
+ACT = mybir.ActivationFunctionType
+ALU = mybir.AluOpType
+
+P = 128
+PACK = 4
+PASSES = 2
+BANK = 512
+HALVES = S // BANK
+SLICES = PASSES * PACK
+UNITS = SLICES * HALVES
+QUADS = 4
+RUN = 8
+BLOCKS = P // RUN
+
+ROUND_BASE = 1.5 * 2.0**16
+ROUND_BITS = float((127 + 16) * 2**23 + 2**22)
+ROUND_STEP = 128.0
+
+
+def tile_list_brick_zone_selection_kernel(
+    tc, tab_words, tab_scales, offs, offs2, offs3, offs4, w4_words, w4_scales, b1, w2, b2, page0, wgs, zg, pairm, out
+):
+    nc = tc.nc
+    with ExitStack() as ctx:
+        keep = ctx.enter_context(tc.tile_pool(name="keep", bufs=1))
+        big = ctx.enter_context(tc.tile_pool(name="big", bufs=2))
+        ring = ctx.enter_context(tc.tile_pool(name="ring", bufs=2))
+        pages = ctx.enter_context(tc.tile_pool(name="pages", bufs=5))
+        psum = ctx.enter_context(tc.psum_pool(name="psum", bufs=2))
+
+        def load_list(name, src):
+            tile = keep.tile(list(src.shape), U16, name=name)
+            nc.sync.dma_start(tile[:], src)
+            return tile
+
+        tab_planes = keep.tile([P, PASSES, T], U8, name="tab_planes", align_bytes=64)
+        nc.vector.memset(tab_planes[:, 0, :].bitcast(I32), 0)
+        nc.gpsimd.memset(tab_planes[:, 1, :].bitcast(I32), 0)
+        for quad in range(QUADS):
+            nc.sync.dma_start(
+                tab_planes[32 * quad : 32 * quad + 4, :, :].bitcast(I32),
+                tab_scales[:, 4 * quad : 4 * quad + 4, :].rearrange("a r t -> r a t").bitcast(I32),
+            )
+        ident = keep.tile([P, P], F32, name="ident")
+        make_identity(nc, ident[:])
+
+        vec_rows = keep.tile([6, BANK], F32, name="vec_rows")
+        for n, vec in enumerate((b1, b2, zg)):
+            nc.sync.dma_start(vec_rows[2 * n : 2 * n + 2, :], vec.rearrange("(b c) -> b c", b=PASSES))
+        idx = load_list("idx", offs)
+        w4_planes_raw = keep.tile([P, PASSES, H // 4], I32, name="w4_planes_raw", align_bytes=64)
+
+        def load_w4_scales(quad):
+            nc.sync.dma_start(
+                w4_planes_raw[32 * quad : 32 * quad + 4, :, :],
+                w4_scales[:, 4 * quad : 4 * quad + 4, :].rearrange("a r c -> r a c").bitcast(I32),
+            )
+
+        for quad in range(QUADS - 1):
+            load_w4_scales(quad)
+        tab = []
+        for a in range(PASSES):
+            tab.append(big.tile([P, T], I32, name=f"tab{a}", tag="big", align_bytes=64))
+        nc.sync.dma_start(tab[0][:], tab_words[0].rearrange("p t i -> p (t i)").bitcast(I32))
+        load_w4_scales(QUADS - 1)
+        w4_raw = keep.tile([P, PASSES, H // 2], I32, name="w4_raw", align_bytes=64)
+        nc.sync.dma_start(w4_raw[:], w4_words.rearrange("a p c -> p a c").bitcast(I32))
+        nc.sync.dma_start(tab[1][:], tab_words[1].rearrange("p t i -> p (t i)").bitcast(I32))
+
+        w2_raw = {}
+
+        def load_w2(b, tiles):
+            for a in range(PASSES):
+                w2_raw[(a, b)] = tiles[a]
+                rows = w2[a * 512 : (a + 1) * 512, b * BANK : (b + 1) * BANK]
+                nc.sync.dma_start(tiles[a], rows.rearrange("(p j) c -> p j c", j=PACK))
+
+        w2_first = [keep.tile([P, PACK, BANK], F32, name=f"w2_first{a}") for a in range(PASSES)]
+        load_w2(0, [tile[:] for tile in w2_first])
+
+        page_rows = page0.rearrange("(b q t i) c -> b t q i c", b=PASSES, q=BLOCKS, t=PACK)
+        page = {}
+
+        def load_page(s):
+            page[s] = pages.tile([P, T2], F32, name=f"page{s}", tag="page")
+            nc.sync.dma_start(page[s][:], page_rows[s // PACK, s % PACK])
+
+        wgs_rows = wgs.rearrange("(c t i) j -> t c i j", t=PACK, i=RUN)
+        wgs_dealt = {}
+
+        def load_wgs(t):
+            wgs_dealt[t] = keep.tile([P, S], F32, name=f"wgs{t}")
+            for quad in (0, 2, 1, 3):
+                nc.sync.dma_start(wgs_dealt[t][32 * quad : 32 * quad + 32, :], wgs_rows[t])
+
+        idx2 = load_list("idx2", offs2)
+        load_page(0)
+        load_wgs(0)
+        idx4 = load_list("idx4", offs4)
+        idx3 = load_list("idx3", offs3)
+
+        minus_base = keep.tile([P, P], F32, name="minus_base")
+        nc.vector.memset(minus_base[:], -ROUND_BASE)
+        quarter = keep.tile([P, 1], F32, name="quarter")
+        nc.vector.memset(quarter[:], 0.25)
+        half_pi = keep.tile([P, 1], F32, name="half_pi")
+        nc.vector.tensor_scalar(half_pi[:], quarter[:], 2.0 * math.pi, None, ALU.mult)
+
+        w4_planes = keep.tile([P, PASSES * SLICES, BLOCKS * 2], I32, name="w4_planes", align_bytes=64)
+        nc.vector.memset(w4_planes[:], 0)
+        vec_dealt = keep.tile([P, PACK, P], F32, name="vec_dealt")
+        nc.vector.memset(vec_dealt[:], 0.0)
+        nc.vector.tensor_copy(
+            vec_dealt[0:6, :, :].rearrange("n t (q i) -> n t q i", i=RUN),
+            vec_rows[:].rearrange("n (q t i) -> n t q i", t=PACK, i=RUN),
+        )
+        vec_bank = psum.tile([P, PACK, P], F32, name="vec_bank", tag="frac")
+        for t in range(PACK):
+            nc.tensor.transpose(vec_bank[:, t, :], vec_dealt[:, t, :], ident[:])
+        b1_turns = keep.tile([P, PACK, PASSES], F32, name="b1_turns")
+        nc.vector.tensor_scalar(b1_turns[:], vec_bank[:, :, 0:2], 0.5 / math.pi, None, ALU.mult)
+        b2_zg = keep.tile([P, PACK, 2 * PASSES], F32, name="b2_zg")
+        nc.vector.tensor_copy(b2_zg[:], vec_bank[:, :, 2:6])
+
+        def half_of(listed, h):
+            cols = BANK // 16
+            return listed[:, h * cols : (h + 1) * cols]
+
+        for quad in range(QUADS):
+            rows = slice(32 * quad, 32 * quad + 4)
+            nc.vector.tensor_copy(
+                w4_planes[rows].rearrange("p (g t) (q w) -> p g t q w", t=PACK, w=2),
+                w4_planes_raw[rows].rearrange("p a (b q t w) -> p (a b) t q w", b=PASSES, t=PACK, w=2),
+            )
+        v_first = keep.tile([P, S], U32, name="v_first", align_bytes=64)
+        nc.vector.tensor_copy(v_first[:], tab[0][:].bitcast(U32).indirect(idx[:]))
+        v_planes = {}
+
+        def gather_planes(h):
+            for a in range(PASSES):
+                v_planes[(a, h)] = keep.tile([P, BANK], U8, name=f"v_plane{a}_{h}", align_bytes=64)
+                nc.vector.tensor_copy(v_planes[(a, h)][:], tab_planes[:, a, :].indirect(half_of(idx, h)))
+
+        v_second = [keep.tile([P, BANK], U32, name=f"v_second{h}", align_bytes=64) for h in range(HALVES)]
+
+        def v_operand(a, h):
+            words = v_first[:, h * BANK : (h + 1) * BANK] if a == 0 else v_second[h][:]
+            return words.bitcast(FP8X4), v_planes[(a, h)][:]
+
+        gather_planes(0)
+        w4_source = w4_raw[:].rearrange("p a (b q t w) -> p a b t q w", b=PASSES, t=PACK, w=4)
+        w4_lead = keep.tile([P, PASSES, BLOCKS, 4], I32, name="w4_lead", align_bytes=64)
+        nc.vector.tensor_copy(w4_lead[:], w4_source[:, :, 0, 0])
+        gather_planes(1)
+        for h in range(HALVES):
+            nc.vector.tensor_copy(v_second[h][:], tab[1][:].bitcast(U32).indirect(half_of(idx, h)))
+        w4_rest = keep.tile([P, PASSES, SLICES, BLOCKS, 4], I32, name="w4_rest", align_bytes=64)
+        nc.gpsimd.tensor_copy(w4_rest[:, :, 1:PACK], w4_source[:, :, 0, 1:PACK])
+        nc.gpsimd.tensor_copy(w4_rest[:, :, PACK:SLICES], w4_source[:, :, 1])
+
+        def w4_operand(a, s):
+            words = w4_lead[:, a] if s == 0 else w4_rest[:, a, s]
+            return words.rearrange("p q w -> p (q w)").bitcast(U8).bitcast(FP4X4)
+
+        w2_codes, w2_planes = {}, {}
+
+        def quantize_w2(s):
+            b, t = divmod(s, PACK)
+            grouped = keep.tile([P, PASSES, P, PACK], BF16, name="w2_grouped", tag="w2_grouped", align_bytes=64)
+            copier = nc.vector.tensor_copy if s == 0 else nc.scalar.copy
+            for a in range(PASSES):
+                copier(
+                    grouped[:, a, :, :].rearrange("p (q i) j -> p q i j", i=RUN),
+                    w2_raw[(a, b)].rearrange("p j (q t i) -> p t q i j", t=PACK, i=RUN)[:, t],
+                )
+            if s == 0:
+                w2_codes[s] = keep.tile([P, PASSES, P], U32, name="w2_codes", tag="turns0", align_bytes=64)
+            else:
+                w2_codes[s] = ring.tile([P, PASSES, P], U32, name="w2_codes", align_bytes=64, bufs=3)
+            w2_planes[s] = ring.tile([P, PASSES, P], U8, name="w2_planes", align_bytes=64, bufs=3)
+            nc.vector.quantize_mx(
+                out=w2_codes[s][:].rearrange("p a m -> p (a m)").bitcast(FP8X4),
+                scales=w2_planes[s][:].rearrange("p a m -> p (a m)"),
+                in_=grouped[:].rearrange("p a m j -> p (a m j)"),
+            )
+
+        turns, whole, folded, cosine, value = {}, {}, {}, {}, {}
+
+        def angle(u):
+            s, h = divmod(u, HALVES)
+            b, t = divmod(s, PACK)
+            bank = psum.tile([P, BANK], F32, name="ang", tag="ang")
+            for a in range(PASSES):
+                nc.tensor.matmul_mx(
+                    out=bank[:],
+                    lhsT=w4_operand(a, s),
+                    lhsT_scale=w4_planes[:, a * SLICES + s, :].bitcast(U8),
+                    rhs=v_operand(a, h)[0],
+                    rhs_scale=v_operand(a, h)[1],
+                    start=(a == 0),
+                    stop=(a == PASSES - 1),
+                )
+            turns[u] = keep.tile([P, BANK], F32, name="turns", tag=f"turns{u % 2}", align_bytes=64)
+            if s == 0:
+                nc.vector.tensor_scalar(
+                    turns[u][:], bank[:], 0.5 / math.pi, b1_turns[:, t, b : b + 1], ALU.mult, ALU.add
+                )
+                whole[u] = ring.tile([P, BANK], I32, name="whole", tag="whole")
+                nc.vector.tensor_scalar(whole[u][:], turns[u][:], -ROUND_STEP, ROUND_BITS, ALU.mult, ALU.add)
+                return
+            nc.scalar.activation(
+                turns[u][:], bank[:], ACT.Identity, bias=b1_turns[:, t, b : b + 1], scale=0.5 / math.pi
+            )
+            whole[u] = ring.tile([P, BANK], U32, name="whole", tag="whole")
+            nc.scalar.activation(whole[u][:], turns[u][:], ACT.Copy, bias=ROUND_BITS, scale=-ROUND_STEP)
+
+        def reduce_turns(u):
+            if u < HALVES:
+                fraction = ring.tile([P, BANK], F32, name="fraction")
+                nc.vector.scalar_tensor_tensor(
+                    fraction[:], whole[u][:].bitcast(F32), -ROUND_BASE, turns[u][:], ALU.add, ALU.add
+                )
+                folded[u] = keep.tile([P, BANK], F32, name="folded", tag=f"folded{u % 2}")
+                nc.scalar.activation(folded[u][:], fraction[:], ACT.Abs)
+                return
+            bank = psum.tile([P, BANK], F32, name="frac", tag="frac")
+            for c in range(BANK // P):
+                cols = slice(c * P, (c + 1) * P)
+                terms = (whole[u][:, cols].bitcast(F32), minus_base[:], turns[u][:, cols])
+                for n, term in enumerate(terms):
+                    nc.tensor.matmul(
+                        bank[:, cols], term, ident[:], is_transpose=True, start=(n == 0), stop=(n == len(terms) - 1)
+                    )
+            folded[u] = keep.tile([P, BANK], F32, name="folded", tag=f"folded{u % 2}")
+            nc.scalar.activation(folded[u][:], bank[:], ACT.Abs)
+
+        def cos_and_value(u):
+            s, h = divmod(u, HALVES)
+            bank = folded[u]
+            if s > 0:
+                bank = psum.tile([P, BANK], F32, name="back", tag="back")
+                for c in range(BANK // P):
+                    cols = slice(c * P, (c + 1) * P)
+                    nc.tensor.transpose(bank[:, cols], folded[u][:, cols], ident[:])
+            if h == 0:
+                cosine[s] = keep.tile([P, HALVES, BANK], F32, name="cosine", tag=f"cos_or_picks{s % 2}")
+            nc.scalar.activation(cosine[s][:, h, :], bank[:], ACT.Sin, bias=half_pi[:], scale=-2.0 * math.pi)
+            value[u] = psum.tile([P, BANK], F32, name="val", tag="val")
+            for a in range(PASSES):
+                nc.tensor.matmul_mx(
+                    out=value[u][:],
+                    lhsT=w2_codes[s][:, a, :].bitcast(FP8X4),
+                    lhsT_scale=w2_planes[s][:, a, :],
+                    rhs=v_operand(a, h)[0],
+                    rhs_scale=v_operand(a, h)[1],
+                    start=(a == 0),
+                    stop=(a == PASSES - 1),
+                )
+
+        feature = {}
+
+        def multiply(u):
+            s, h = divmod(u, HALVES)
+            b, t = divmod(s, PACK)
+            if h == 0:
+                feature[s] = ring.tile([P, HALVES, BANK], F32, name="feature")
+            nc.vector.scalar_tensor_tensor(
+                feature[s][:, h, :], value[u][:], b2_zg[:, t, b : b + 1], cosine[s][:, h, :], ALU.add, ALU.mult
+            )
+
+        def scatter(s):
+            weights = wgs_dealt[s % PACK]
+            if s == 0:
+                for h in range(HALVES):
+                    cols = slice(h * BANK, (h + 1) * BANK)
+                    nc.vector.tensor_tensor(
+                        page[s][:].indirect(half_of(idx2, h)), feature[s][:, h, :], weights[:, cols], ALU.mult
+                    )
+            else:
+                nc.vector.tensor_tensor(
+                    page[s][:].indirect(idx2[:]), feature[s][:].rearrange("p h c -> p (h c)"), weights[:], ALU.mult
+                )
+
+        x1_rows = [keep.tile([P, PACK, PICKS], BF16, name=f"x1_rows{b}") for b in range(PASSES)]
+        x2_rows = [keep.tile([P, PACK, PICKS], BF16, name=f"x2_rows{b}") for b in range(PASSES)]
+        zones = {}
+
+        def fetch(s):
+            b, t = divmod(s, PACK)
+            zones[s] = keep.tile([P, PICKS], F32, name="zones", tag=f"cos_or_picks{(s + 1) % 2}")
+            nc.vector.tensor_copy(zones[s][:], page[s][:].indirect(idx4[:]))
+            nc.vector.tensor_copy(x1_rows[b][:, t, :], page[s][:].indirect(idx3[:]))
+
+        def weigh_zones(s):
+            b, t = divmod(s, PACK)
+            magnitude = keep.tile([P, PICKS], F32, name="magnitude", tag="folded1")
+            nc.scalar.activation(magnitude[:], zones[s][:], ACT.Abs)
+            nc.scalar.activation(
+                x2_rows[b][:, t, :], magnitude[:], ACT.Copy, scale=b2_zg[:, t, PASSES + b : PASSES + b + 1]
+            )
+
+        x_codes, x_planes = {}, {}
+
+        def quantize_x(name, rows, b, copiers):
+            x_codes[(name, b)] = keep.tile([P, PICKS], U32, name=f"{name}_codes{b}", align_bytes=64)
+            x_planes[(name, b)] = keep.tile([P, PICKS], U8, name=f"{name}_planes{b}", align_bytes=64)
+            width = PICKS // len(copiers)
+            for n, copier in enumerate(copiers):
+                cols = slice(n * width, (n + 1) * width)
+                grouped = ring.tile([P, width, PACK], BF16, name="x_grouped", tag="x_grouped", align_bytes=64, bufs=3)
+                copier(grouped[:], rows[:, :, cols].rearrange("p t m -> p m t"))
+                nc.vector.quantize_mx(
+                    out=x_codes[(name, b)][:, cols].bitcast(FP8X4),
+                    scales=x_planes[(name, b)][:, cols],
+                    in_=grouped[:].rearrange("p m t -> p (m t)"),
+                )
+
+        pair_tile = {}
+
+        def later_loads(s):
+            if s + 1 < SLICES:
+                if s + 1 < PACK:
+                    load_wgs(s + 1)
+                load_page(s + 1)
+            if s == 1:
+                second = big.tile([P, PASSES, PACK, BANK], F32, name="w2_second", tag="big", align_bytes=64)
+                load_w2(1, [second[:, a] for a in range(PASSES)])
+            if s == 2:
+                pair_tile[0] = big.tile([P, PICKS // P, PICKS], F32, name="pair", tag="big", align_bytes=64)
+                nc.sync.dma_start(pair_tile[0][:], pairm.rearrange("(c p) j -> p c j", p=P))
+
+        for u in range(HALVES):
+            angle(u)
+            reduce_turns(u)
+        quantize_w2(0)
+        for u in range(HALVES):
+            cos_and_value(u)
+            multiply(u)
+        scatter(0)
+        later_loads(0)
+        for step in range(HALVES, UNITS + 2):
+            if step < UNITS:
+                angle(step)
+            if step % HALVES == 1:
+                later_loads(step // HALVES)
+                if step // HALVES < SLICES:
+                    quantize_w2(step // HALVES)
+            if HALVES <= step - 1 < UNITS:
+                reduce_turns(step - 1)
+            if HALVES <= step - 2 < UNITS:
+                cos_and_value(step - 2)
+                multiply(step - 2)
+                s, h = divmod(step - 2, HALVES)
+                if h == HALVES - 1:
+                    fetch(s - 1)
+                    scatter(s)
+                    if s > 1:
+                        weigh_zones(s - 2)
+        weigh_zones(SLICES - 2)
+        quantize_x("x1", x1_rows[0], 0, [nc.scalar.copy])
+        quantize_x("x2", x2_rows[0], 0, [nc.scalar.copy])
+        fetch(SLICES - 1)
+        weigh_zones(SLICES - 1)
+        quantize_x("x1", x1_rows[1], 1, [nc.vector.tensor_copy])
+        quantize_x("x2", x2_rows[1], 1, [nc.vector.tensor_copy, nc.scalar.copy])
+
+        tags = ("ang", "frac", "back", "val")
+        scores = [psum.tile([P, PICKS], F32, name=f"scores{c}", tag=tags[c]) for c in range(PICKS // P)]
+        for b in range(PASSES):
+            for c in range(PICKS // P):
+                cols = slice(c * P, (c + 1) * P)
+                nc.tensor.matmul_mx(
+                    out=scores[c][:],
+                    lhsT=x_codes[("x1", b)][:, cols].bitcast(FP8X4),
+                    lhsT_scale=x_planes[("x1", b)][:, cols],
+                    rhs=x_codes[("x2", b)][:].bitcast(FP8X4),
+                    rhs_scale=x_planes[("x2", b)][:],
+                    start=(b == 0),
+                    stop=(b == PASSES - 1),
+                )
+        for c in range(PICKS // P):
+            result = ring.tile([P, PICKS], F32, name="result", bufs=4)
+            nc.vector.tensor_tensor(result[:], scores[c][:], pair_tile[0][:, c, :], ALU.add)
+            nc.sync.dma_start(out[c * P : (c + 1) * P, :], result[:])

@@ -43,7 +43,7 @@ def tile_list_brick_zone_selection_kernel(
         big = ctx.enter_context(tc.tile_pool(name="big", bufs=2))
         ring = ctx.enter_context(tc.tile_pool(name="ring", bufs=2))
         pages = ctx.enter_context(tc.tile_pool(name="pages", bufs=5))
-        psum = ctx.enter_context(tc.psum_pool(name="psum", bufs=2))
+        psum = ctx.enter_context(tc.psum_pool(name="psum", bufs=4))
 
         def load_list(name, src):
             tile = keep.tile(list(src.shape), U16, name=name)
@@ -116,8 +116,6 @@ def tile_list_brick_zone_selection_kernel(
         idx4 = load_list("idx4", offs4)
         idx3 = load_list("idx3", offs3)
 
-        minus_base = keep.tile([P, P], F32, name="minus_base")
-        nc.vector.memset(minus_base[:], -ROUND_BASE)
         quarter = keep.tile([P, 1], F32, name="quarter")
         nc.vector.memset(quarter[:], 0.25)
         half_pi = keep.tile([P, 1], F32, name="half_pi")
@@ -131,7 +129,7 @@ def tile_list_brick_zone_selection_kernel(
             vec_dealt[0:6, :, :].rearrange("n t (q i) -> n t q i", i=RUN),
             vec_rows[:].rearrange("n (q t i) -> n t q i", t=PACK, i=RUN),
         )
-        vec_bank = psum.tile([P, PACK, P], F32, name="vec_bank", tag="frac")
+        vec_bank = psum.tile([P, PACK, P], F32, name="vec_bank", tag="ang")
         for t in range(PACK):
             nc.tensor.transpose(vec_bank[:, t, :], vec_dealt[:, t, :], ident[:])
         b1_turns = keep.tile([P, PACK, PASSES], F32, name="b1_turns")
@@ -184,9 +182,8 @@ def tile_list_brick_zone_selection_kernel(
         def quantize_w2(s):
             b, t = divmod(s, PACK)
             grouped = keep.tile([P, PASSES, P, PACK], BF16, name="w2_grouped", tag="w2_grouped", align_bytes=64)
-            copier = nc.vector.tensor_copy if s == 0 else nc.scalar.copy
             for a in range(PASSES):
-                copier(
+                nc.scalar.copy(
                     grouped[:, a, :, :].rearrange("p (q i) j -> p q i j", i=RUN),
                     w2_raw[(a, b)].rearrange("p j (q t i) -> p t q i j", t=PACK, i=RUN)[:, t],
                 )
@@ -201,7 +198,7 @@ def tile_list_brick_zone_selection_kernel(
                 in_=grouped[:].rearrange("p a m j -> p (a m j)"),
             )
 
-        turns, whole, folded, cosine, value = {}, {}, {}, {}, {}
+        turns, whole, cosine = {}, {}, {}
 
         def angle(u):
             s, h = divmod(u, HALVES)
@@ -217,55 +214,43 @@ def tile_list_brick_zone_selection_kernel(
                     start=(a == 0),
                     stop=(a == PASSES - 1),
                 )
-            turns[u] = keep.tile([P, BANK], F32, name="turns", tag=f"turns{u % 2}", align_bytes=64)
-            if s == 0:
-                nc.vector.tensor_scalar(
-                    turns[u][:], bank[:], 0.5 / math.pi, b1_turns[:, t, b : b + 1], ALU.mult, ALU.add
-                )
-                whole[u] = ring.tile([P, BANK], I32, name="whole", tag="whole")
-                nc.vector.tensor_scalar(whole[u][:], turns[u][:], -ROUND_STEP, ROUND_BITS, ALU.mult, ALU.add)
-                return
-            nc.scalar.activation(
-                turns[u][:], bank[:], ACT.Identity, bias=b1_turns[:, t, b : b + 1], scale=0.5 / math.pi
-            )
-            whole[u] = ring.tile([P, BANK], U32, name="whole", tag="whole")
-            nc.scalar.activation(whole[u][:], turns[u][:], ACT.Copy, bias=ROUND_BITS, scale=-ROUND_STEP)
-
-        def reduce_turns(u):
-            if u < HALVES:
-                fraction = ring.tile([P, BANK], F32, name="fraction")
-                nc.vector.scalar_tensor_tensor(
-                    fraction[:], whole[u][:].bitcast(F32), -ROUND_BASE, turns[u][:], ALU.add, ALU.add
-                )
-                folded[u] = keep.tile([P, BANK], F32, name="folded", tag=f"folded{u % 2}")
-                nc.scalar.activation(folded[u][:], fraction[:], ACT.Abs)
-                return
-            bank = psum.tile([P, BANK], F32, name="frac", tag="frac")
-            for c in range(BANK // P):
-                cols = slice(c * P, (c + 1) * P)
-                terms = (whole[u][:, cols].bitcast(F32), minus_base[:], turns[u][:, cols])
-                for n, term in enumerate(terms):
-                    nc.tensor.matmul(
-                        bank[:, cols], term, ident[:], is_transpose=True, start=(n == 0), stop=(n == len(terms) - 1)
-                    )
-            folded[u] = keep.tile([P, BANK], F32, name="folded", tag=f"folded{u % 2}")
-            nc.scalar.activation(folded[u][:], bank[:], ACT.Abs)
-
-        def cos_and_value(u):
-            s, h = divmod(u, HALVES)
-            bank = folded[u]
-            if s > 0:
-                bank = psum.tile([P, BANK], F32, name="back", tag="back")
-                for c in range(BANK // P):
-                    cols = slice(c * P, (c + 1) * P)
-                    nc.tensor.transpose(bank[:, cols], folded[u][:, cols], ident[:])
+            turns[u] = keep.tile([P, BANK], F32, name="turns", tag=f"turns{h}", align_bytes=64)
             if h == 0:
-                cosine[s] = keep.tile([P, HALVES, BANK], F32, name="cosine", tag=f"cos_or_picks{s % 2}")
-            nc.scalar.activation(cosine[s][:, h, :], bank[:], ACT.Sin, bias=half_pi[:], scale=-2.0 * math.pi)
-            value[u] = psum.tile([P, BANK], F32, name="val", tag="val")
+                whole[s] = keep.tile([P, HALVES, BANK], U32, name="whole", tag=f"whole_or_feature{(s + 1) % 2}")
+            offset = b1_turns[:, t, b : b + 1]
+            if s == 0:
+                nc.vector.tensor_scalar(turns[u][:], bank[:], 0.5 / math.pi, offset, ALU.mult, ALU.add)
+                nc.vector.tensor_scalar(
+                    whole[s][:, h, :].bitcast(I32), turns[u][:], -ROUND_STEP, ROUND_BITS, ALU.mult, ALU.add
+                )
+            else:
+                nc.scalar.activation(turns[u][:], bank[:], ACT.Identity, bias=offset, scale=0.5 / math.pi)
+                nc.scalar.activation(whole[s][:, h, :], turns[u][:], ACT.Copy, bias=ROUND_BITS, scale=-ROUND_STEP)
+
+        def cos_of(u):
+            s, h = divmod(u, HALVES)
+            fraction = ring.tile([P, BANK], F32, name="fraction")
+            nc.vector.scalar_tensor_tensor(
+                fraction[:], whole[s][:, h, :].bitcast(F32), -ROUND_BASE, turns[u][:], ALU.add, ALU.add
+            )
+            folded = keep.tile([P, BANK], F32, name="folded", tag=f"folded{h}")
+            if s == 0:
+                nc.vector.scalar_tensor_tensor(folded[:], fraction[:], -1.0, fraction[:], ALU.mult, ALU.max)
+            else:
+                nc.scalar.activation(folded[:], fraction[:], ACT.Abs)
+            if h == 0:
+                cosine[s] = keep.tile([P, HALVES, BANK], F32, name="cosine", tag=f"cos_or_picks{s % 3}")
+            nc.scalar.activation(cosine[s][:, h, :], folded[:], ACT.Sin, bias=half_pi[:], scale=-2.0 * math.pi)
+
+        feature = {}
+
+        def multiply(u):
+            s, h = divmod(u, HALVES)
+            b, t = divmod(s, PACK)
+            value = psum.tile([P, BANK], F32, name="val", tag="val")
             for a in range(PASSES):
                 nc.tensor.matmul_mx(
-                    out=value[u][:],
+                    out=value[:],
                     lhsT=w2_codes[s][:, a, :].bitcast(FP8X4),
                     lhsT_scale=w2_planes[s][:, a, :],
                     rhs=v_operand(a, h)[0],
@@ -273,16 +258,11 @@ def tile_list_brick_zone_selection_kernel(
                     start=(a == 0),
                     stop=(a == PASSES - 1),
                 )
-
-        feature = {}
-
-        def multiply(u):
-            s, h = divmod(u, HALVES)
-            b, t = divmod(s, PACK)
             if h == 0:
-                feature[s] = ring.tile([P, HALVES, BANK], F32, name="feature")
+                tag = "first_feature" if s == 0 else f"whole_or_feature{s % 2}"
+                feature[s] = keep.tile([P, HALVES, BANK], F32, name="feature", tag=tag)
             nc.vector.scalar_tensor_tensor(
-                feature[s][:, h, :], value[u][:], b2_zg[:, t, b : b + 1], cosine[s][:, h, :], ALU.add, ALU.mult
+                feature[s][:, h, :], value[:], b2_zg[:, t, b : b + 1], cosine[s][:, h, :], ALU.add, ALU.mult
             )
 
         def scatter(s):
@@ -304,7 +284,7 @@ def tile_list_brick_zone_selection_kernel(
 
         def fetch(s):
             b, t = divmod(s, PACK)
-            zones[s] = keep.tile([P, PICKS], F32, name="zones", tag=f"cos_or_picks{(s + 1) % 2}")
+            zones[s] = keep.tile([P, PICKS], F32, name="zones", tag=f"cos_or_picks{(s + 1) % 3}")
             nc.vector.tensor_copy(zones[s][:], page[s][:].indirect(idx4[:]))
             nc.vector.tensor_copy(x1_rows[b][:, t, :], page[s][:].indirect(idx3[:]))
 
@@ -346,33 +326,32 @@ def tile_list_brick_zone_selection_kernel(
                 pair_tile[0] = big.tile([P, PICKS // P, PICKS], F32, name="pair", tag="big", align_bytes=64)
                 nc.sync.dma_start(pair_tile[0][:], pairm.rearrange("(c p) j -> p c j", p=P))
 
-        for u in range(HALVES):
-            angle(u)
-            reduce_turns(u)
+        def units(s):
+            return range(HALVES * s, HALVES * (s + 1))
+
+        def cosines(s):
+            for u in units(s):
+                angle(u)
+            for u in units(s):
+                cos_of(u)
+
+        cosines(0)
         quantize_w2(0)
-        for u in range(HALVES):
-            cos_and_value(u)
-            multiply(u)
-        scatter(0)
-        later_loads(0)
-        for step in range(HALVES, UNITS + 2):
-            if step < UNITS:
-                angle(step)
-            if step % HALVES == 1:
-                later_loads(step // HALVES)
-                if step // HALVES < SLICES:
-                    quantize_w2(step // HALVES)
-            if HALVES <= step - 1 < UNITS:
-                reduce_turns(step - 1)
-            if HALVES <= step - 2 < UNITS:
-                cos_and_value(step - 2)
-                multiply(step - 2)
-                s, h = divmod(step - 2, HALVES)
-                if h == HALVES - 1:
-                    fetch(s - 1)
-                    scatter(s)
-                    if s > 1:
-                        weigh_zones(s - 2)
+        for s in range(SLICES):
+            if 0 < s < SLICES - 1:
+                cosines(s + 1)
+            if s > 1:
+                weigh_zones(s - 2)
+            for u in units(s):
+                multiply(u)
+            if s > 0:
+                fetch(s - 1)
+            scatter(s)
+            later_loads(s)
+            if s == 0:
+                cosines(1)
+            if s + 1 < SLICES:
+                quantize_w2(s + 1)
         weigh_zones(SLICES - 2)
         quantize_x("x1", x1_rows[0], 0, [nc.scalar.copy])
         quantize_x("x2", x2_rows[0], 0, [nc.scalar.copy])
@@ -381,7 +360,7 @@ def tile_list_brick_zone_selection_kernel(
         quantize_x("x1", x1_rows[1], 1, [nc.vector.tensor_copy])
         quantize_x("x2", x2_rows[1], 1, [nc.vector.tensor_copy, nc.scalar.copy])
 
-        tags = ("ang", "frac", "back", "val")
+        tags = ("ang", "ang", "val", "val")
         scores = [psum.tile([P, PICKS], F32, name=f"scores{c}", tag=tags[c]) for c in range(PICKS // P)]
         for b in range(PASSES):
             for c in range(PICKS // P):

@@ -26,8 +26,9 @@ HALVES = S // BANK
 SLICES = PASSES * PACK
 UNITS = SLICES * HALVES
 QUADS = 4
-RUN = 8
-BLOCKS = P // RUN
+HEAD = 2
+RUN = 4
+GROUPS = P // RUN
 
 ROUND_BASE = 1.5 * 2.0**16
 ROUND_BITS = float((127 + 16) * 2**23 + 2**22)
@@ -42,7 +43,7 @@ def tile_list_brick_zone_selection_kernel(
         keep = ctx.enter_context(tc.tile_pool(name="keep", bufs=1))
         big = ctx.enter_context(tc.tile_pool(name="big", bufs=2))
         ring = ctx.enter_context(tc.tile_pool(name="ring", bufs=2))
-        pages = ctx.enter_context(tc.tile_pool(name="pages", bufs=5))
+        pages = ctx.enter_context(tc.tile_pool(name="pages", bufs=4))
         psum = ctx.enter_context(tc.psum_pool(name="psum", bufs=4))
 
         def load_list(name, src):
@@ -53,11 +54,9 @@ def tile_list_brick_zone_selection_kernel(
         tab_planes = keep.tile([P, PASSES, T], U8, name="tab_planes", align_bytes=64)
         nc.vector.memset(tab_planes[:, 0, :].bitcast(I32), 0)
         nc.gpsimd.memset(tab_planes[:, 1, :].bitcast(I32), 0)
-        for quad in range(QUADS):
-            nc.sync.dma_start(
-                tab_planes[32 * quad : 32 * quad + 4, :, :].bitcast(I32),
-                tab_scales[:, 4 * quad : 4 * quad + 4, :].rearrange("a r t -> r a t").bitcast(I32),
-            )
+        tab_scale_rows = tab_scales.rearrange("a (q r) t -> r q a t", r=4).bitcast(I32)
+        for row in range(4):
+            nc.sync.dma_start(tab_planes[row:P:32, :, :].bitcast(I32), tab_scale_rows[row])
         ident = keep.tile([P, P], F32, name="ident")
         make_identity(nc, ident[:])
 
@@ -67,35 +66,33 @@ def tile_list_brick_zone_selection_kernel(
         idx = load_list("idx", offs)
         w4_planes_raw = keep.tile([P, PASSES, H // 4], I32, name="w4_planes_raw", align_bytes=64)
 
-        def load_w4_scales(quad):
-            nc.sync.dma_start(
-                w4_planes_raw[32 * quad : 32 * quad + 4, :, :],
-                w4_scales[:, 4 * quad : 4 * quad + 4, :].rearrange("a r c -> r a c").bitcast(I32),
-            )
+        w4_scale_rows = w4_scales.rearrange("a (q r) c -> r q a c", r=4).bitcast(I32)
 
-        for quad in range(QUADS - 1):
-            load_w4_scales(quad)
-        tab = []
-        for a in range(PASSES):
-            tab.append(big.tile([P, T], I32, name=f"tab{a}", tag="big", align_bytes=64))
-        nc.sync.dma_start(tab[0][:], tab_words[0].rearrange("p t i -> p (t i)").bitcast(I32))
-        load_w4_scales(QUADS - 1)
-        w4_raw = keep.tile([P, PASSES, H // 2], I32, name="w4_raw", align_bytes=64)
-        nc.sync.dma_start(w4_raw[:], w4_words.rearrange("a p c -> p a c").bitcast(I32))
-        nc.sync.dma_start(tab[1][:], tab_words[1].rearrange("p t i -> p (t i)").bitcast(I32))
+        def load_w4_scales(row):
+            nc.sync.dma_start(w4_planes_raw[row:P:32, :, :], w4_scale_rows[row])
 
         w2_raw = {}
 
-        def load_w2(b, tiles):
-            for a in range(PASSES):
-                w2_raw[(a, b)] = tiles[a]
-                rows = w2[a * 512 : (a + 1) * 512, b * BANK : (b + 1) * BANK]
-                nc.sync.dma_start(tiles[a], rows.rearrange("(p j) c -> p j c", j=PACK))
+        def load_w2(a, b, tile):
+            w2_raw[(a, b)] = tile
+            rows = w2[a * 512 : (a + 1) * 512, b * BANK : (b + 1) * BANK]
+            nc.sync.dma_start(tile, rows.rearrange("(p j) c -> p j c", j=PACK))
 
         w2_first = [keep.tile([P, PACK, BANK], F32, name=f"w2_first{a}") for a in range(PASSES)]
-        load_w2(0, [tile[:] for tile in w2_first])
+        for quad in range(QUADS - 1):
+            load_w4_scales(quad)
+        tab = [big.tile([P, T], I32, name=f"tab{a}", tag="big", align_bytes=64) for a in range(PASSES)]
+        tab_source = tab_words.rearrange("a p t i -> a p (t i)").bitcast(I32)
+        nc.sync.dma_start(tab[0][:, : T // 2], tab_source[0, :, : T // 2])
+        load_w4_scales(QUADS - 1)
+        nc.sync.dma_start(tab[0][:, T // 2 :], tab_source[0, :, T // 2 :])
+        w4_raw = keep.tile([P, PASSES, H // 2], I32, name="w4_raw", align_bytes=64)
+        nc.sync.dma_start(w4_raw[:], w4_words.rearrange("a p c -> p a c").bitcast(I32))
+        nc.sync.dma_start(tab[1][:], tab_source[1])
+        for a in range(PASSES):
+            load_w2(a, 0, w2_first[a][:])
 
-        page_rows = page0.rearrange("(b q t i) c -> b t q i c", b=PASSES, q=BLOCKS, t=PACK)
+        page_rows = page0.rearrange("(b q t i) c -> b t q i c", b=PASSES, q=GROUPS, t=PACK)
         page = {}
 
         def load_page(s):
@@ -107,8 +104,10 @@ def tile_list_brick_zone_selection_kernel(
 
         def load_wgs(t):
             wgs_dealt[t] = keep.tile([P, S], F32, name=f"wgs{t}")
-            for quad in (0, 2, 1, 3):
-                nc.sync.dma_start(wgs_dealt[t][32 * quad : 32 * quad + 32, :], wgs_rows[t])
+            spans = [slice(0, BANK), slice(BANK, S)] if t == 0 else [slice(0, S)]
+            for cols in spans:
+                for quad in (0, 2, 1, 3):
+                    nc.sync.dma_start(wgs_dealt[t][32 * quad : 32 * quad + 32, cols], wgs_rows[t][:, :, cols])
 
         idx2 = load_list("idx2", offs2)
         load_page(0)
@@ -121,7 +120,7 @@ def tile_list_brick_zone_selection_kernel(
         half_pi = keep.tile([P, 1], F32, name="half_pi")
         nc.vector.tensor_scalar(half_pi[:], quarter[:], 2.0 * math.pi, None, ALU.mult)
 
-        w4_planes = keep.tile([P, PASSES * SLICES, BLOCKS * 2], I32, name="w4_planes", align_bytes=64)
+        w4_planes = keep.tile([P, PASSES * SLICES, GROUPS], I32, name="w4_planes", align_bytes=64)
         nc.vector.memset(w4_planes[:], 0)
         vec_dealt = keep.tile([P, PACK, P], F32, name="vec_dealt")
         nc.vector.memset(vec_dealt[:], 0.0)
@@ -144,65 +143,53 @@ def tile_list_brick_zone_selection_kernel(
         for quad in range(QUADS):
             rows = slice(32 * quad, 32 * quad + 4)
             nc.vector.tensor_copy(
-                w4_planes[rows].rearrange("p (g t) (q w) -> p g t q w", t=PACK, w=2),
-                w4_planes_raw[rows].rearrange("p a (b q t w) -> p (a b) t q w", b=PASSES, t=PACK, w=2),
+                w4_planes[rows].rearrange("p (g t) q -> p g q t", t=PACK),
+                w4_planes_raw[rows].rearrange("p a (b q t) -> p (a b) q t", b=PASSES, t=PACK),
             )
+        v_planes = [keep.tile([P, S], U8, name=f"v_plane{a}", align_bytes=64) for a in range(PASSES)]
+        for a in range(PASSES):
+            nc.vector.tensor_copy(v_planes[a][:], tab_planes[:, a, :].indirect(idx[:]))
         v_first = keep.tile([P, S], U32, name="v_first", align_bytes=64)
         nc.vector.tensor_copy(v_first[:], tab[0][:].bitcast(U32).indirect(idx[:]))
-        v_planes = {}
-
-        def gather_planes(h):
-            for a in range(PASSES):
-                v_planes[(a, h)] = keep.tile([P, BANK], U8, name=f"v_plane{a}_{h}", align_bytes=64)
-                nc.vector.tensor_copy(v_planes[(a, h)][:], tab_planes[:, a, :].indirect(half_of(idx, h)))
-
+        w4_dealt = keep.tile([P, PASSES * SLICES, GROUPS * 2], I32, name="w4_dealt", align_bytes=64)
+        nc.vector.tensor_copy(
+            w4_dealt[:].rearrange("p (g t) (q w) -> p g t q w", t=PACK, w=2),
+            w4_raw[:].rearrange("p a (b q t w) -> p (a b) t q w", b=PASSES, t=PACK, w=2),
+        )
         v_second = [keep.tile([P, BANK], U32, name=f"v_second{h}", align_bytes=64) for h in range(HALVES)]
-
-        def v_operand(a, h):
-            words = v_first[:, h * BANK : (h + 1) * BANK] if a == 0 else v_second[h][:]
-            return words.bitcast(FP8X4), v_planes[(a, h)][:]
-
-        gather_planes(0)
-        w4_source = w4_raw[:].rearrange("p a (b q t w) -> p a b t q w", b=PASSES, t=PACK, w=4)
-        w4_lead = keep.tile([P, PASSES, BLOCKS, 4], I32, name="w4_lead", align_bytes=64)
-        nc.vector.tensor_copy(w4_lead[:], w4_source[:, :, 0, 0])
-        gather_planes(1)
         for h in range(HALVES):
             nc.vector.tensor_copy(v_second[h][:], tab[1][:].bitcast(U32).indirect(half_of(idx, h)))
-        w4_rest = keep.tile([P, PASSES, SLICES, BLOCKS, 4], I32, name="w4_rest", align_bytes=64)
-        nc.gpsimd.tensor_copy(w4_rest[:, :, 1:PACK], w4_source[:, :, 0, 1:PACK])
-        nc.gpsimd.tensor_copy(w4_rest[:, :, PACK:SLICES], w4_source[:, :, 1])
+
+        def v_operand(a, h):
+            cols = slice(h * BANK, (h + 1) * BANK)
+            words = v_first[:, cols] if a == 0 else v_second[h][:]
+            return words.bitcast(FP8X4), v_planes[a][:, cols]
 
         def w4_operand(a, s):
-            words = w4_lead[:, a] if s == 0 else w4_rest[:, a, s]
-            return words.rearrange("p q w -> p (q w)").bitcast(U8).bitcast(FP4X4)
+            return w4_dealt[:, a * SLICES + s, :].bitcast(U8).bitcast(FP4X4)
 
         w2_codes, w2_planes = {}, {}
 
-        def quantize_w2(s):
-            b, t = divmod(s, PACK)
-            grouped = keep.tile([P, PASSES, P, PACK], BF16, name="w2_grouped", tag="w2_grouped", align_bytes=64)
-            for a in range(PASSES):
-                nc.scalar.copy(
-                    grouped[:, a, :, :].rearrange("p (q i) j -> p q i j", i=RUN),
-                    w2_raw[(a, b)].rearrange("p j (q t i) -> p t q i j", t=PACK, i=RUN)[:, t],
-                )
-            if s == 0:
-                w2_codes[s] = keep.tile([P, PASSES, P], U32, name="w2_codes", tag="turns0", align_bytes=64)
-            else:
-                w2_codes[s] = ring.tile([P, PASSES, P], U32, name="w2_codes", align_bytes=64, bufs=3)
-            w2_planes[s] = ring.tile([P, PASSES, P], U8, name="w2_planes", align_bytes=64, bufs=3)
+        def quantize_w2(first, count):
+            grouped = ring.tile([P, count, PASSES, P, PACK], BF16, name="w2_grouped", align_bytes=64)
+            codes = ring.tile([P, count, PASSES, P], U32, name="w2_codes", align_bytes=64, bufs=3)
+            planes = ring.tile([P, count, PASSES, P], U8, name="w2_planes", align_bytes=64, bufs=3)
+            for n in range(count):
+                b, t = divmod(first + n, PACK)
+                for a in range(PASSES):
+                    nc.scalar.copy(
+                        grouped[:, n, a, :, :].rearrange("p (q i) j -> p q i j", i=RUN),
+                        w2_raw[(a, b)].rearrange("p j (q t i) -> p t q i j", t=PACK, i=RUN)[:, t],
+                    )
+                w2_codes[first + n], w2_planes[first + n] = codes[:, n], planes[:, n]
             nc.vector.quantize_mx(
-                out=w2_codes[s][:].rearrange("p a m -> p (a m)").bitcast(FP8X4),
-                scales=w2_planes[s][:].rearrange("p a m -> p (a m)"),
-                in_=grouped[:].rearrange("p a m j -> p (a m j)"),
+                out=codes[:].rearrange("p n a m -> p (n a m)").bitcast(FP8X4),
+                scales=planes[:].rearrange("p n a m -> p (n a m)"),
+                in_=grouped[:].rearrange("p n a m j -> p (n a m j)"),
             )
-
-        turns, whole, cosine = {}, {}, {}
 
         def angle(u):
             s, h = divmod(u, HALVES)
-            b, t = divmod(s, PACK)
             bank = psum.tile([P, BANK], F32, name="ang", tag="ang")
             for a in range(PASSES):
                 nc.tensor.matmul_mx(
@@ -214,33 +201,67 @@ def tile_list_brick_zone_selection_kernel(
                     start=(a == 0),
                     stop=(a == PASSES - 1),
                 )
-            turns[u] = keep.tile([P, BANK], F32, name="turns", tag=f"turns{h}", align_bytes=64)
-            if h == 0:
-                whole[s] = keep.tile([P, HALVES, BANK], U32, name="whole", tag=f"whole_or_feature{(s + 1) % 2}")
-            offset = b1_turns[:, t, b : b + 1]
-            if s == 0:
-                nc.vector.tensor_scalar(turns[u][:], bank[:], 0.5 / math.pi, offset, ALU.mult, ALU.add)
-                nc.vector.tensor_scalar(
-                    whole[s][:, h, :].bitcast(I32), turns[u][:], -ROUND_STEP, ROUND_BITS, ALU.mult, ALU.add
-                )
-            else:
-                nc.scalar.activation(turns[u][:], bank[:], ACT.Identity, bias=offset, scale=0.5 / math.pi)
-                nc.scalar.activation(whole[s][:, h, :], turns[u][:], ACT.Copy, bias=ROUND_BITS, scale=-ROUND_STEP)
+            return bank
 
-        def cos_of(u):
-            s, h = divmod(u, HALVES)
-            fraction = ring.tile([P, BANK], F32, name="fraction")
-            nc.vector.scalar_tensor_tensor(
-                fraction[:], whole[s][:, h, :].bitcast(F32), -ROUND_BASE, turns[u][:], ALU.add, ALU.add
-            )
-            folded = keep.tile([P, BANK], F32, name="folded", tag=f"folded{h}")
+        cosine = {}
+        shared = keep.tile([P, SLICES * BANK], F32, name="shared")
+        x1_rows = shared[:].bitcast(BF16).rearrange("p (n c) -> p n c", n=SLICES)[:, 1:, 0:PICKS]
+
+        turns, whole, nearest = {}, {}, {}
+        spans = [slice(h * BANK, (h + 1) * BANK) for h in range(HALVES)]
+
+        def count_turns(s):
+            b, t = divmod(s, PACK)
+            offset = b1_turns[:, t, b : b + 1]
+            turns[s] = keep.tile([P, S], F32, name="turns", tag=f"turns{s % 2}", align_bytes=64)
+            whole[s] = keep.tile([P, S], U32, name="whole")
+            for h, cols in enumerate(spans):
+                bank = angle(HALVES * s + h)
+                if s == 0:
+                    nc.vector.tensor_scalar(turns[s][:, cols], bank[:], 0.5 / math.pi, offset, ALU.mult, ALU.add)
+                else:
+                    nc.scalar.activation(turns[s][:, cols], bank[:], ACT.Identity, bias=offset, scale=0.5 / math.pi)
             if s == 0:
-                nc.vector.scalar_tensor_tensor(folded[:], fraction[:], -1.0, fraction[:], ALU.mult, ALU.max)
+                for cols in spans:
+                    nc.vector.tensor_scalar(
+                        whole[s][:, cols].bitcast(I32), turns[s][:, cols], -ROUND_STEP, ROUND_BITS, ALU.mult, ALU.add
+                    )
             else:
-                nc.scalar.activation(folded[:], fraction[:], ACT.Abs)
-            if h == 0:
-                cosine[s] = keep.tile([P, HALVES, BANK], F32, name="cosine", tag=f"cos_or_picks{s % 3}")
-            nc.scalar.activation(cosine[s][:, h, :], folded[:], ACT.Sin, bias=half_pi[:], scale=-2.0 * math.pi)
+                nc.scalar.activation(whole[s][:], turns[s][:], ACT.Copy, bias=ROUND_BITS, scale=-ROUND_STEP)
+            if s >= HEAD:
+                nearest[s] = ring.tile([P, S], F32, name="nearest", tag="nearest")
+                nc.scalar.activation(nearest[s][:], whole[s][:].bitcast(F32), ACT.Copy, bias=-ROUND_BASE, scale=1.0)
+
+        def cosines(s):
+            if s < HEAD:
+                fraction = ring.tile([P, S], F32, name="fraction", tag="nearest")
+            else:
+                fraction = keep.tile([P, S], F32, name="fraction", tag=f"feature{s % 2}")
+            folded = keep.tile([P, S], F32, name="folded", tag="folded")
+            first_half = keep.tile([P, BANK], F32, name="cosine", tag=f"cos_or_picks{s % 3}")
+            cosine[s] = [first_half[:], shared[:, s * BANK : (s + 1) * BANK]]
+            for cols in spans if s == 0 else [slice(0, S)]:
+                if s < HEAD:
+                    nc.vector.scalar_tensor_tensor(
+                        fraction[:, cols],
+                        whole[s][:, cols].bitcast(F32),
+                        -ROUND_BASE,
+                        turns[s][:, cols],
+                        ALU.add,
+                        ALU.add,
+                    )
+                else:
+                    nc.gpsimd.tensor_tensor(fraction[:], nearest[s][:], turns[s][:], ALU.add)
+                if s == 0:
+                    nc.vector.scalar_tensor_tensor(
+                        folded[:, cols], fraction[:, cols], -1.0, fraction[:, cols], ALU.mult, ALU.max
+                    )
+                else:
+                    nc.scalar.activation(folded[:, cols], fraction[:, cols], ACT.Abs)
+                for h in range(cols.start // BANK, cols.stop // BANK):
+                    nc.scalar.activation(
+                        cosine[s][h], folded[:, spans[h]], ACT.Sin, bias=half_pi[:], scale=-2.0 * math.pi
+                    )
 
         feature = {}
 
@@ -259,10 +280,9 @@ def tile_list_brick_zone_selection_kernel(
                     stop=(a == PASSES - 1),
                 )
             if h == 0:
-                tag = "first_feature" if s == 0 else f"whole_or_feature{s % 2}"
-                feature[s] = keep.tile([P, HALVES, BANK], F32, name="feature", tag=tag)
+                feature[s] = keep.tile([P, HALVES, BANK], F32, name="feature", tag=f"feature{s % 2}")
             nc.vector.scalar_tensor_tensor(
-                feature[s][:, h, :], value[:], b2_zg[:, t, b : b + 1], cosine[s][:, h, :], ALU.add, ALU.mult
+                feature[s][:, h, :], value[:], b2_zg[:, t, b : b + 1], cosine[s][h], ALU.add, ALU.mult
             )
 
         def scatter(s):
@@ -278,39 +298,38 @@ def tile_list_brick_zone_selection_kernel(
                     page[s][:].indirect(idx2[:]), feature[s][:].rearrange("p h c -> p (h c)"), weights[:], ALU.mult
                 )
 
-        x1_rows = [keep.tile([P, PACK, PICKS], BF16, name=f"x1_rows{b}") for b in range(PASSES)]
-        x2_rows = [keep.tile([P, PACK, PICKS], BF16, name=f"x2_rows{b}") for b in range(PASSES)]
+        x2_rows = keep.tile([P, PACK, PICKS], BF16, name="x2_rows")
+        last = {}
         zones = {}
 
         def fetch(s):
-            b, t = divmod(s, PACK)
             zones[s] = keep.tile([P, PICKS], F32, name="zones", tag=f"cos_or_picks{(s + 1) % 3}")
             nc.vector.tensor_copy(zones[s][:], page[s][:].indirect(idx4[:]))
-            nc.vector.tensor_copy(x1_rows[b][:, t, :], page[s][:].indirect(idx3[:]))
+            target = x1_rows[:, s, :] if s < SLICES - 2 else last["x1"][:, :, s - PACK]
+            nc.vector.tensor_copy(target, page[s][:].indirect(idx3[:]))
 
         def weigh_zones(s):
             b, t = divmod(s, PACK)
-            magnitude = keep.tile([P, PICKS], F32, name="magnitude", tag="folded1")
+            magnitude = keep.tile([P, PICKS], F32, name="magnitude", tag="folded")
             nc.scalar.activation(magnitude[:], zones[s][:], ACT.Abs)
-            nc.scalar.activation(
-                x2_rows[b][:, t, :], magnitude[:], ACT.Copy, scale=b2_zg[:, t, PASSES + b : PASSES + b + 1]
-            )
+            target = x2_rows[:, t, :] if b == 0 else last["x2"][:, :, t]
+            nc.scalar.activation(target, magnitude[:], ACT.Copy, scale=b2_zg[:, t, PASSES + b : PASSES + b + 1])
 
         x_codes, x_planes = {}, {}
 
-        def quantize_x(name, rows, b, copiers):
+        def quantize_x(name, b, grouped):
             x_codes[(name, b)] = keep.tile([P, PICKS], U32, name=f"{name}_codes{b}", align_bytes=64)
             x_planes[(name, b)] = keep.tile([P, PICKS], U8, name=f"{name}_planes{b}", align_bytes=64)
-            width = PICKS // len(copiers)
-            for n, copier in enumerate(copiers):
-                cols = slice(n * width, (n + 1) * width)
-                grouped = ring.tile([P, width, PACK], BF16, name="x_grouped", tag="x_grouped", align_bytes=64, bufs=3)
-                copier(grouped[:], rows[:, :, cols].rearrange("p t m -> p m t"))
-                nc.vector.quantize_mx(
-                    out=x_codes[(name, b)][:, cols].bitcast(FP8X4),
-                    scales=x_planes[(name, b)][:, cols],
-                    in_=grouped[:].rearrange("p m t -> p (m t)"),
-                )
+            nc.vector.quantize_mx(
+                out=x_codes[(name, b)][:].bitcast(FP8X4),
+                scales=x_planes[(name, b)][:],
+                in_=grouped[:].rearrange("p m t -> p (m t)"),
+            )
+
+        def interleave_and_quantize(name, rows):
+            grouped = ring.tile([P, PICKS, PACK], BF16, name="x_grouped", align_bytes=64)
+            nc.scalar.copy(grouped[:], rows.rearrange("p t m -> p m t"))
+            quantize_x(name, 0, grouped)
 
         pair_tile = {}
 
@@ -319,9 +338,10 @@ def tile_list_brick_zone_selection_kernel(
                 if s + 1 < PACK:
                     load_wgs(s + 1)
                 load_page(s + 1)
-            if s == 1:
+            if s == 0:
                 second = big.tile([P, PASSES, PACK, BANK], F32, name="w2_second", tag="big", align_bytes=64)
-                load_w2(1, [second[:, a] for a in range(PASSES)])
+                for a in range(PASSES):
+                    load_w2(a, 1, second[:, a])
             if s == 2:
                 pair_tile[0] = big.tile([P, PICKS // P, PICKS], F32, name="pair", tag="big", align_bytes=64)
                 nc.sync.dma_start(pair_tile[0][:], pairm.rearrange("(c p) j -> p c j", p=P))
@@ -329,36 +349,42 @@ def tile_list_brick_zone_selection_kernel(
         def units(s):
             return range(HALVES * s, HALVES * (s + 1))
 
-        def cosines(s):
-            for u in units(s):
-                angle(u)
-            for u in units(s):
-                cos_of(u)
-
+        quantize_w2(0, 1)
+        count_turns(0)
         cosines(0)
-        quantize_w2(0)
+        count_turns(1)
+        cosines(1)
+        quantize_w2(1, 1)
+        count_turns(2)
         for s in range(SLICES):
-            if 0 < s < SLICES - 1:
-                cosines(s + 1)
-            if s > 1:
-                weigh_zones(s - 2)
             for u in units(s):
                 multiply(u)
             if s > 0:
                 fetch(s - 1)
+            if 0 < s < SLICES - 1:
+                cosines(s + 1)
+            if 0 < s < SLICES - 2:
+                count_turns(s + 2)
+            if s == SLICES - 2:
+                for n, name in enumerate(("x2", "x1")):
+                    last[name] = keep.tile([P, PICKS, PACK], BF16, name="last", tag=f"turns{n}", align_bytes=64)
+            if s > 1:
+                weigh_zones(s - 2)
+            if s == SLICES - 2:
+                nc.scalar.copy(last["x1"][:, :, 0:2], x1_rows[:, PACK : PACK + 2, :].rearrange("p t m -> p m t"))
             scatter(s)
             later_loads(s)
             if s == 0:
-                cosines(1)
-            if s + 1 < SLICES:
-                quantize_w2(s + 1)
+                quantize_w2(2, 2)
+            if s in (1, 3):
+                quantize_w2(s + 3, 2)
         weigh_zones(SLICES - 2)
-        quantize_x("x1", x1_rows[0], 0, [nc.scalar.copy])
-        quantize_x("x2", x2_rows[0], 0, [nc.scalar.copy])
+        interleave_and_quantize("x1", x1_rows[:, 0:PACK, :])
+        interleave_and_quantize("x2", x2_rows[:])
         fetch(SLICES - 1)
         weigh_zones(SLICES - 1)
-        quantize_x("x1", x1_rows[1], 1, [nc.vector.tensor_copy])
-        quantize_x("x2", x2_rows[1], 1, [nc.vector.tensor_copy, nc.scalar.copy])
+        quantize_x("x1", 1, last["x1"])
+        quantize_x("x2", 1, last["x2"])
 
         tags = ("ang", "ang", "val", "val")
         scores = [psum.tile([P, PICKS], F32, name=f"scores{c}", tag=tags[c]) for c in range(PICKS // P)]

@@ -27,6 +27,7 @@ SLICES = PASSES * PACK
 UNITS = SLICES * HALVES
 QUADS = 4
 HEAD = 2
+SPLIT = 384
 RUN = 4
 GROUPS = P // RUN
 
@@ -207,16 +208,20 @@ def tile_list_brick_zone_selection_kernel(
         shared = keep.tile([P, SLICES * BANK], F32, name="shared")
         x1_rows = shared[:].bitcast(BF16).rearrange("p (n c) -> p n c", n=SLICES)[:, 1:, 0:PICKS]
 
-        turns, whole, nearest = {}, {}, {}
+        turns, whole, nearest, first_bank = {}, {}, {}, {}
         spans = [slice(h * BANK, (h + 1) * BANK) for h in range(HALVES)]
+
+        shares = [slice(0, SPLIT), slice(SPLIT, S)]
 
         def count_turns(s):
             b, t = divmod(s, PACK)
             offset = b1_turns[:, t, b : b + 1]
             turns[s] = keep.tile([P, S], F32, name="turns", tag=f"turns{s % 2}", align_bytes=64)
-            whole[s] = keep.tile([P, S], U32, name="whole")
+            whole[s] = keep.tile([P, S], U32, name="whole", tag="whole", align_bytes=64)
             for h, cols in enumerate(spans):
                 bank = angle(HALVES * s + h)
+                if h == 0:
+                    first_bank[s] = bank
                 if s == 0:
                     nc.vector.tensor_scalar(turns[s][:, cols], bank[:], 0.5 / math.pi, offset, ALU.mult, ALU.add)
                 else:
@@ -229,39 +234,57 @@ def tile_list_brick_zone_selection_kernel(
             else:
                 nc.scalar.activation(whole[s][:], turns[s][:], ACT.Copy, bias=ROUND_BITS, scale=-ROUND_STEP)
             if s >= HEAD:
-                nearest[s] = ring.tile([P, S], F32, name="nearest", tag="nearest")
-                nc.scalar.activation(nearest[s][:], whole[s][:].bitcast(F32), ACT.Copy, bias=-ROUND_BASE, scale=1.0)
+                nearest[s] = [
+                    keep.tile([P, SPLIT], F32, name="nearest_low", tag=f"feature{(s + 1) % 2}"),
+                    ring.tile([P, S - SPLIT], F32, name="nearest_high"),
+                ]
+                for part, cols in zip(nearest[s], shares):
+                    nc.scalar.activation(
+                        part[:], whole[s][:, cols].bitcast(F32), ACT.Copy, bias=-ROUND_BASE, scale=1.0
+                    )
 
-        def cosines(s):
+        fraction = {}
+
+        def subtract_whole(s):
+            fraction[s] = keep.tile([P, S], F32, name="fraction", tag="fraction" if s < HEAD else f"feature{s % 2}")
             if s < HEAD:
-                fraction = ring.tile([P, S], F32, name="fraction", tag="nearest")
-            else:
-                fraction = keep.tile([P, S], F32, name="fraction", tag=f"feature{s % 2}")
-            folded = keep.tile([P, S], F32, name="folded", tag="folded")
-            first_half = keep.tile([P, BANK], F32, name="cosine", tag=f"cos_or_picks{s % 3}")
-            cosine[s] = [first_half[:], shared[:, s * BANK : (s + 1) * BANK]]
-            for cols in spans if s == 0 else [slice(0, S)]:
-                if s < HEAD:
+                for cols in spans if s == 0 else [slice(0, S)]:
                     nc.vector.scalar_tensor_tensor(
-                        fraction[:, cols],
+                        fraction[s][:, cols],
                         whole[s][:, cols].bitcast(F32),
                         -ROUND_BASE,
                         turns[s][:, cols],
                         ALU.add,
                         ALU.add,
                     )
-                else:
-                    nc.gpsimd.tensor_tensor(fraction[:], nearest[s][:], turns[s][:], ALU.add)
-                if s == 0:
+            else:
+                low, high = shares
+                nc.gpsimd.tensor_tensor(fraction[s][:, high], nearest[s][1][:], turns[s][:, high], ALU.add)
+                nc.vector.scalar_tensor_tensor(
+                    fraction[s][:, low], first_bank[s][:, low], 0.5 / math.pi, nearest[s][0][:], ALU.mult, ALU.add
+                )
+
+        def cosines(s):
+            if s < SLICES - 1:
+                folded = keep.tile([P, S], F32, name="folded", tag="folded")
+            else:
+                folded = keep.tile([P, S], F32, name="folded", tag="whole", align_bytes=64)
+            first_half = keep.tile([P, BANK], F32, name="cosine", tag=f"cos_or_picks{s % 3}")
+            cosine[s] = [first_half[:], shared[:, s * BANK : (s + 1) * BANK]]
+            if s == 0:
+                for cols in spans:
                     nc.vector.scalar_tensor_tensor(
-                        folded[:, cols], fraction[:, cols], -1.0, fraction[:, cols], ALU.mult, ALU.max
+                        folded[:, cols], fraction[s][:, cols], -1.0, fraction[s][:, cols], ALU.mult, ALU.max
                     )
-                else:
-                    nc.scalar.activation(folded[:, cols], fraction[:, cols], ACT.Abs)
-                for h in range(cols.start // BANK, cols.stop // BANK):
-                    nc.scalar.activation(
-                        cosine[s][h], folded[:, spans[h]], ACT.Sin, bias=half_pi[:], scale=-2.0 * math.pi
-                    )
+            elif s < HEAD:
+                nc.scalar.activation(folded[:], fraction[s][:], ACT.Abs)
+            else:
+                low, high = shares
+                b, t = divmod(s, PACK)
+                nc.scalar.activation(folded[:, low], fraction[s][:, low], ACT.Abs, bias=b1_turns[:, t, b : b + 1])
+                nc.scalar.activation(folded[:, high], fraction[s][:, high], ACT.Abs)
+            for h, cols in enumerate(spans):
+                nc.scalar.activation(cosine[s][h], folded[:, cols], ACT.Sin, bias=half_pi[:], scale=-2.0 * math.pi)
 
         feature = {}
 
@@ -350,12 +373,11 @@ def tile_list_brick_zone_selection_kernel(
             return range(HALVES * s, HALVES * (s + 1))
 
         quantize_w2(0, 1)
-        count_turns(0)
-        cosines(0)
-        count_turns(1)
-        cosines(1)
+        for s in range(HEAD):
+            count_turns(s)
+            subtract_whole(s)
+            cosines(s)
         quantize_w2(1, 1)
-        count_turns(2)
         for s in range(SLICES):
             for u in units(s):
                 multiply(u)
@@ -363,16 +385,18 @@ def tile_list_brick_zone_selection_kernel(
                 fetch(s - 1)
             if 0 < s < SLICES - 1:
                 cosines(s + 1)
-            if 0 < s < SLICES - 2:
+            if s < SLICES - 2:
                 count_turns(s + 2)
             if s == SLICES - 2:
-                for n, name in enumerate(("x2", "x1")):
-                    last[name] = keep.tile([P, PICKS, PACK], BF16, name="last", tag=f"turns{n}", align_bytes=64)
+                for name, tag in (("x2", "turns0"), ("x1", "whole")):
+                    last[name] = keep.tile([P, PICKS, PACK], BF16, name="last", tag=tag, align_bytes=64)
             if s > 1:
                 weigh_zones(s - 2)
             if s == SLICES - 2:
                 nc.scalar.copy(last["x1"][:, :, 0:2], x1_rows[:, PACK : PACK + 2, :].rearrange("p t m -> p m t"))
             scatter(s)
+            if s < SLICES - 2:
+                subtract_whole(s + 2)
             later_loads(s)
             if s == 0:
                 quantize_w2(2, 2)

import math
from contextlib import ExitStack

import concourse.mybir as mybir
from concourse.masks import make_identity

K, H, T, S, T2, PICKS = 1024, 1024, 4096, 1024, 2048, 512
FLOPS = 2 * (2 * K * H * S + H * PICKS * PICKS)

F32 = mybir.dt.float32
BF16 = mybir.dt.bfloat16
I32 = mybir.dt.int32
U32 = mybir.dt.uint32
U16 = mybir.dt.uint16
U8 = mybir.dt.uint8
FP8X4 = mybir.dt.float8_e4m3fn_x4
FP4X4 = mybir.dt.float4_e2m1fn_x4
ACT = mybir.ActivationFunctionType
ALU = mybir.AluOpType

P = 128
PACK = 4
PASSES = 2
BANK = 512
HALVES = S // BANK
SLICES = PASSES * PACK
UNITS = SLICES * HALVES
QUADS = 4
HEAD = 2
SPLIT = 384
RUN = 4
GROUPS = P // RUN

ROUND_BASE = 1.5 * 2.0**16
ROUND_BITS = float((127 + 16) * 2**23 + 2**22)
ROUND_STEP = 128.0


def tile_list_brick_zone_selection_kernel(
    tc, tab_words, tab_scales, offs, offs2, offs3, offs4, w4_words, w4_scales, b1, w2, b2, page0, wgs, zg, pairm, out
):
    nc = tc.nc
    with ExitStack() as ctx:
        keep = ctx.enter_context(tc.tile_pool(name="keep", bufs=1))
        big = ctx.enter_context(tc.tile_pool(name="big", bufs=2))
        ring = ctx.enter_context(tc.tile_pool(name="ring", bufs=2))
        pages = ctx.enter_context(tc.tile_pool(name="pages", bufs=4))
        psum = ctx.enter_context(tc.psum_pool(name="psum", bufs=4))

        def load_list(name, src):
            tile = keep.tile(list(src.shape), U16, name=name)
            nc.sync.dma_start(tile[:], src)
            return tile

        tab_planes = keep.tile([P, PASSES, T], U8, name="tab_planes", align_bytes=64)
        nc.vector.memset(tab_planes[:, 0, :].bitcast(I32), 0)
        nc.gpsimd.memset(tab_planes[:, 1, :].bitcast(I32), 0)
        tab_scale_rows = tab_scales.rearrange("a (q r) t -> r q a t", r=4).bitcast(I32)
        for row in range(4):
            nc.sync.dma_start(tab_planes[row:P:32, :, :].bitcast(I32), tab_scale_rows[row])
        ident = keep.tile([P, P], F32, name="ident")
        make_identity(nc, ident[:])

        vec_rows = keep.tile([6, BANK], F32, name="vec_rows")
        for n, vec in enumerate((b1, b2, zg)):
            nc.sync.dma_start(vec_rows[2 * n : 2 * n + 2, :], vec.rearrange("(b c) -> b c", b=PASSES))
        idx = load_list("idx", offs)
        w4_planes_raw = keep.tile([P, PASSES, H // 4], I32, name="w4_planes_raw", align_bytes=64)

        w4_scale_rows = w4_scales.rearrange("a (q r) c -> r q a c", r=4).bitcast(I32)

        def load_w4_scales(row):
            nc.sync.dma_start(w4_planes_raw[row:P:32, :, :], w4_scale_rows[row])

        w2_raw = {}

        def load_w2(a, b, tile):
            w2_raw[(a, b)] = tile
            rows = w2[a * 512 : (a + 1) * 512, b * BANK : (b + 1) * BANK]
            nc.sync.dma_start(tile, rows.rearrange("(p j) c -> p j c", j=PACK))

        w2_first = [keep.tile([P, PACK, BANK], F32, name=f"w2_first{a}") for a in range(PASSES)]
        for quad in range(QUADS - 1):
            load_w4_scales(quad)
        tab = [big.tile([P, T], I32, name=f"tab{a}", tag="big", align_bytes=64) for a in range(PASSES)]
        tab_source = tab_words.rearrange("a p t i -> a p (t i)").bitcast(I32)
        nc.sync.dma_start(tab[0][:, : T // 2], tab_source[0, :, : T // 2])
        load_w4_scales(QUADS - 1)
        nc.sync.dma_start(tab[0][:, T // 2 :], tab_source[0, :, T // 2 :])
        w4_raw = keep.tile([P, PASSES, H // 2], I32, name="w4_raw", align_bytes=64)
        nc.sync.dma_start(w4_raw[:], w4_words.rearrange("a p c -> p a c").bitcast(I32))
        nc.sync.dma_start(tab[1][:], tab_source[1])
        for a in range(PASSES):
            load_w2(a, 0, w2_first[a][:])

        page_rows = page0.rearrange("(b q t i) c -> b t q i c", b=PASSES, q=GROUPS, t=PACK)
        page = {}

        def load_page(s):
            page[s] = pages.tile([P, T2], F32, name=f"page{s}", tag="page")
            nc.sync.dma_start(page[s][:], page_rows[s // PACK, s % PACK])

        wgs_rows = wgs.rearrange("(c t i) j -> t c i j", t=PACK, i=RUN)
        wgs_dealt = {}

        def load_wgs(t):
            wgs_dealt[t] = keep.tile([P, S], F32, name=f"wgs{t}")
            spans = [slice(0, BANK), slice(BANK, S)] if t == 0 else [slice(0, S)]
            for cols in spans:
                for quad in (0, 2, 1, 3):
                    nc.sync.dma_start(wgs_dealt[t][32 * quad : 32 * quad + 32, cols], wgs_rows[t][:, :, cols])

        idx2 = load_list("idx2", offs2)
        load_page(0)
        load_wgs(0)
        idx4 = load_list("idx4", offs4)
        idx3 = load_list("idx3", offs3)

        quarter = keep.tile([P, 1], F32, name="quarter")
        nc.vector.memset(quarter[:], 0.25)
        half_pi = keep.tile([P, 1], F32, name="half_pi")
        nc.vector.tensor_scalar(half_pi[:], quarter[:], 2.0 * math.pi, None, ALU.mult)

        w4_planes = keep.tile([P, PASSES * SLICES, GROUPS], I32, name="w4_planes", align_bytes=64)
        nc.vector.memset(w4_planes[:], 0)
        vec_dealt = keep.tile([P, PACK, P], F32, name="vec_dealt")
        nc.vector.memset(vec_dealt[:], 0.0)
        nc.vector.tensor_copy(
            vec_dealt[0:6, :, :].rearrange("n t (q i) -> n t q i", i=RUN),
            vec_rows[:].rearrange("n (q t i) -> n t q i", t=PACK, i=RUN),
        )
        vec_bank = psum.tile([P, PACK, P], F32, name="vec_bank", tag="ang")
        for t in range(PACK):
            nc.tensor.transpose(vec_bank[:, t, :], vec_dealt[:, t, :], ident[:])
        b1_turns = keep.tile([P, PACK, PASSES], F32, name="b1_turns")
        nc.vector.tensor_scalar(b1_turns[:], vec_bank[:, :, 0:2], 0.5 / math.pi, None, ALU.mult)
        b2_zg = keep.tile([P, PACK, 2 * PASSES], F32, name="b2_zg")
        nc.vector.tensor_copy(b2_zg[:], vec_bank[:, :, 2:6])

        def half_of(listed, h):
            cols = BANK // 16
            return listed[:, h * cols : (h + 1) * cols]

        for quad in range(QUADS):
            rows = slice(32 * quad, 32 * quad + 4)
            nc.vector.tensor_copy(
                w4_planes[rows].rearrange("p (g t) q -> p g q t", t=PACK),
                w4_planes_raw[rows].rearrange("p a (b q t) -> p (a b) q t", b=PASSES, t=PACK),
            )
        v_planes = [keep.tile([P, S], U8, name=f"v_plane{a}", align_bytes=64) for a in range(PASSES)]
        for a in range(PASSES):
            nc.vector.tensor_copy(v_planes[a][:], tab_planes[:, a, :].indirect(idx[:]))
        v_first = keep.tile([P, S], U32, name="v_first", align_bytes=64)
        nc.vector.tensor_copy(v_first[:], tab[0][:].bitcast(U32).indirect(idx[:]))
        w4_dealt = keep.tile([P, PASSES * SLICES, GROUPS * 2], I32, name="w4_dealt", align_bytes=64)
        nc.vector.tensor_copy(
            w4_dealt[:].rearrange("p (g t) (q w) -> p g t q w", t=PACK, w=2),
            w4_raw[:].rearrange("p a (b q t w) -> p (a b) t q w", b=PASSES, t=PACK, w=2),
        )
        v_second = [keep.tile([P, BANK], U32, name=f"v_second{h}", align_bytes=64) for h in range(HALVES)]
        for h in range(HALVES):
            nc.vector.tensor_copy(v_second[h][:], tab[1][:].bitcast(U32).indirect(half_of(idx, h)))

        def v_operand(a, h):
            cols = slice(h * BANK, (h + 1) * BANK)
            words = v_first[:, cols] if a == 0 else v_second[h][:]
            return words.bitcast(FP8X4), v_planes[a][:, cols]

        def w4_operand(a, s):
            return w4_dealt[:, a * SLICES + s, :].bitcast(U8).bitcast(FP4X4)

        w2_codes, w2_planes = {}, {}

        def quantize_w2(first, count):
            grouped = ring.tile([P, count, PASSES, P, PACK], BF16, name="w2_grouped", align_bytes=64)
            codes = ring.tile([P, count, PASSES, P], U32, name="w2_codes", align_bytes=64, bufs=3)
            planes = ring.tile([P, count, PASSES, P], U8, name="w2_planes", align_bytes=64, bufs=3)
            for n in range(count):
                b, t = divmod(first + n, PACK)
                for a in range(PASSES):
                    nc.scalar.copy(
                        grouped[:, n, a, :, :].rearrange("p (q i) j -> p q i j", i=RUN),
                        w2_raw[(a, b)].rearrange("p j (q t i) -> p t q i j", t=PACK, i=RUN)[:, t],
                    )
                w2_codes[first + n], w2_planes[first + n] = codes[:, n], planes[:, n]
            nc.vector.quantize_mx(
                out=codes[:].rearrange("p n a m -> p (n a m)").bitcast(FP8X4),
                scales=planes[:].rearrange("p n a m -> p (n a m)"),
                in_=grouped[:].rearrange("p n a m j -> p (n a m j)"),
            )

        def angle(u):
            s, h = divmod(u, HALVES)
            bank = psum.tile([P, BANK], F32, name="ang", tag="ang")
            for a in range(PASSES):
                nc.tensor.matmul_mx(
                    out=bank[:],
                    lhsT=w4_operand(a, s),
                    lhsT_scale=w4_planes[:, a * SLICES + s, :].bitcast(U8),
                    rhs=v_operand(a, h)[0],
                    rhs_scale=v_operand(a, h)[1],
                    start=(a == 0),
                    stop=(a == PASSES - 1),
                )
            return bank

        cosine = {}
        shared = keep.tile([P, SLICES * BANK], F32, name="shared")
        x1_rows = shared[:].bitcast(BF16).rearrange("p (n c) -> p n c", n=SLICES)[:, 1:, 0:PICKS]

        turns, whole, nearest, first_bank = {}, {}, {}, {}
        spans = [slice(h * BANK, (h + 1) * BANK) for h in range(HALVES)]

        shares = [slice(0, SPLIT), slice(SPLIT, S)]

        def count_turns(s):
            b, t = divmod(s, PACK)
            offset = b1_turns[:, t, b : b + 1]
            turns[s] = keep.tile([P, S], F32, name="turns", tag=f"turns{s % 2}", align_bytes=64)
            whole[s] = keep.tile([P, S], U32, name="whole", tag="whole", align_bytes=64)
            for h, cols in enumerate(spans):
                bank = angle(HALVES * s + h)
                if h == 0:
                    first_bank[s] = bank
                if s == 0:
                    nc.vector.tensor_scalar(turns[s][:, cols], bank[:], 0.5 / math.pi, offset, ALU.mult, ALU.add)
                else:
                    nc.scalar.activation(turns[s][:, cols], bank[:], ACT.Identity, bias=offset, scale=0.5 / math.pi)
            if s == 0:
                for cols in spans:
                    nc.vector.tensor_scalar(
                        whole[s][:, cols].bitcast(I32), turns[s][:, cols], -ROUND_STEP, ROUND_BITS, ALU.mult, ALU.add
                    )
            else:
                nc.scalar.activation(whole[s][:], turns[s][:], ACT.Copy, bias=ROUND_BITS, scale=-ROUND_STEP)
            if s >= HEAD:
                nearest[s] = [
                    keep.tile([P, SPLIT], F32, name="nearest_low", tag=f"feature{(s + 1) % 2}"),
                    ring.tile([P, S - SPLIT], F32, name="nearest_high"),
                ]
                for part, cols in zip(nearest[s], shares):
                    nc.scalar.activation(
                        part[:], whole[s][:, cols].bitcast(F32), ACT.Copy, bias=-ROUND_BASE, scale=1.0
                    )

        fraction = {}

        def subtract_whole(s):
            fraction[s] = keep.tile([P, S], F32, name="fraction", tag="fraction" if s < HEAD else f"feature{s % 2}")
            if s < HEAD:
                for cols in spans if s == 0 else [slice(0, S)]:
                    nc.vector.scalar_tensor_tensor(
                        fraction[s][:, cols],
                        whole[s][:, cols].bitcast(F32),
                        -ROUND_BASE,
                        turns[s][:, cols],
                        ALU.add,
                        ALU.add,
                    )
            else:
                low, high = shares
                nc.gpsimd.tensor_tensor(fraction[s][:, high], nearest[s][1][:], turns[s][:, high], ALU.add)
                nc.vector.scalar_tensor_tensor(
                    fraction[s][:, low], first_bank[s][:, low], 0.5 / math.pi, nearest[s][0][:], ALU.mult, ALU.add
                )

        def cosines(s):
            if s < SLICES - 1:
                folded = keep.tile([P, S], F32, name="folded", tag="folded")
            else:
                folded = keep.tile([P, S], F32, name="folded", tag="whole", align_bytes=64)
            first_half = keep.tile([P, BANK], F32, name="cosine", tag=f"cos_or_picks{s % 3}")
            cosine[s] = [first_half[:], shared[:, s * BANK : (s + 1) * BANK]]
            if s == 0:
                for cols in spans:
                    nc.vector.scalar_tensor_tensor(
                        folded[:, cols], fraction[s][:, cols], -1.0, fraction[s][:, cols], ALU.mult, ALU.max
                    )
            elif s < HEAD:
                nc.scalar.activation(folded[:], fraction[s][:], ACT.Abs)
            else:
                low, high = shares
                b, t = divmod(s, PACK)
                nc.scalar.activation(folded[:, low], fraction[s][:, low], ACT.Abs, bias=b1_turns[:, t, b : b + 1])
                nc.scalar.activation(folded[:, high], fraction[s][:, high], ACT.Abs)
            for h, cols in enumerate(spans):
                nc.scalar.activation(cosine[s][h], folded[:, cols], ACT.Sin, bias=half_pi[:], scale=-2.0 * math.pi)

        feature = {}

        def multiply(u):
            s, h = divmod(u, HALVES)
            b, t = divmod(s, PACK)
            value = psum.tile([P, BANK], F32, name="val", tag="val")
            for a in range(PASSES):
                nc.tensor.matmul_mx(
                    out=value[:],
                    lhsT=w2_codes[s][:, a, :].bitcast(FP8X4),
                    lhsT_scale=w2_planes[s][:, a, :],
                    rhs=v_operand(a, h)[0],
                    rhs_scale=v_operand(a, h)[1],
                    start=(a == 0),
                    stop=(a == PASSES - 1),
                )
            if h == 0:
                feature[s] = keep.tile([P, HALVES, BANK], F32, name="feature", tag=f"feature{s % 2}")
            nc.vector.scalar_tensor_tensor(
                feature[s][:, h, :], value[:], b2_zg[:, t, b : b + 1], cosine[s][h], ALU.add, ALU.mult
            )

        def scatter(s):
            weights = wgs_dealt[s % PACK]
            if s == 0:
                for h in range(HALVES):
                    cols = slice(h * BANK, (h + 1) * BANK)
                    nc.vector.tensor_tensor(
                        page[s][:].indirect(half_of(idx2, h)), feature[s][:, h, :], weights[:, cols], ALU.mult
                    )
            else:
                nc.vector.tensor_tensor(
                    page[s][:].indirect(idx2[:]), feature[s][:].rearrange("p h c -> p (h c)"), weights[:], ALU.mult
                )

        x2_rows = keep.tile([P, PACK, PICKS], BF16, name="x2_rows")
        last = {}
        zones = {}

        def fetch(s):
            zones[s] = keep.tile([P, PICKS], F32, name="zones", tag=f"cos_or_picks{(s + 1) % 3}")
            nc.vector.tensor_copy(zones[s][:], page[s][:].indirect(idx4[:]))
            target = x1_rows[:, s, :] if s < SLICES - 2 else last["x1"][:, :, s - PACK]
            nc.vector.tensor_copy(target, page[s][:].indirect(idx3[:]))

        def weigh_zones(s):
            b, t = divmod(s, PACK)
            magnitude = keep.tile([P, PICKS], F32, name="magnitude", tag="folded")
            nc.scalar.activation(magnitude[:], zones[s][:], ACT.Abs)
            target = x2_rows[:, t, :] if b == 0 else last["x2"][:, :, t]
            nc.scalar.activation(target, magnitude[:], ACT.Copy, scale=b2_zg[:, t, PASSES + b : PASSES + b + 1])

        x_codes, x_planes = {}, {}

        def quantize_x(name, b, grouped):
            x_codes[(name, b)] = keep.tile([P, PICKS], U32, name=f"{name}_codes{b}", align_bytes=64)
            x_planes[(name, b)] = keep.tile([P, PICKS], U8, name=f"{name}_planes{b}", align_bytes=64)
            nc.vector.quantize_mx(
                out=x_codes[(name, b)][:].bitcast(FP8X4),
                scales=x_planes[(name, b)][:],
                in_=grouped[:].rearrange("p m t -> p (m t)"),
            )

        def interleave_and_quantize(name, rows):
            grouped = ring.tile([P, PICKS, PACK], BF16, name="x_grouped", align_bytes=64)
            nc.scalar.copy(grouped[:], rows.rearrange("p t m -> p m t"))
            quantize_x(name, 0, grouped)

        pair_tile = {}

        def later_loads(s):
            if s + 1 < SLICES:
                if s + 1 < PACK:
                    load_wgs(s + 1)
                load_page(s + 1)
            if s == 0:
                second = big.tile([P, PASSES, PACK, BANK], F32, name="w2_second", tag="big", align_bytes=64)
                for a in range(PASSES):
                    load_w2(a, 1, second[:, a])
            if s == 2:
                pair_tile[0] = big.tile([P, PICKS // P, PICKS], F32, name="pair", tag="big", align_bytes=64)
                nc.sync.dma_start(pair_tile[0][:], pairm.rearrange("(c p) j -> p c j", p=P))

        def units(s):
            return range(HALVES * s, HALVES * (s + 1))

        quantize_w2(0, 1)
        for s in range(HEAD):
            count_turns(s)
            subtract_whole(s)
            cosines(s)
        quantize_w2(1, 1)
        for s in range(SLICES):
            for u in units(s):
                multiply(u)
            if s > 0:
                fetch(s - 1)
            if 0 < s < SLICES - 1:
                cosines(s + 1)
            if s < SLICES - 2:
                count_turns(s + 2)
            if s == SLICES - 2:
                for name, tag in (("x2", "turns0"), ("x1", "whole")):
                    last[name] = keep.tile([P, PICKS, PACK], BF16, name="last", tag=tag, align_bytes=64)
            if s > 1:
                weigh_zones(s - 2)
            if s == SLICES - 2:
                nc.scalar.copy(last["x1"][:, :, 0:2], x1_rows[:, PACK : PACK + 2, :].rearrange("p t m -> p m t"))
            scatter(s)
            if s < SLICES - 2:
                subtract_whole(s + 2)
            later_loads(s)
            if s == 0:
                quantize_w2(2, 2)
            if s in (1, 3):
                quantize_w2(s + 3, 2)
        weigh_zones(SLICES - 2)
        interleave_and_quantize("x1", x1_rows[:, 0:PACK, :])
        interleave_and_quantize("x2", x2_rows[:])
        fetch(SLICES - 1)
        weigh_zones(SLICES - 1)
        quantize_x("x1", 1, last["x1"])
        quantize_x("x2", 1, last["x2"])

        tags = ("ang", "ang", "val", "val")
        scores = [psum.tile([P, PICKS], F32, name=f"scores{c}", tag=tags[c]) for c in range(PICKS // P)]
        for b in range(PASSES):
            for c in range(PICKS // P):
                cols = slice(c * P, (c + 1) * P)
                nc.tensor.matmul_mx(
                    out=scores[c][:],
                    lhsT=x_codes[("x1", b)][:, cols].bitcast(FP8X4),
                    lhsT_scale=x_planes[("x1", b)][:, cols],
                    rhs=x_codes[("x2", b)][:].bitcast(FP8X4),
                    rhs_scale=x_planes[("x2", b)][:],
                    start=(b == 0),
                    stop=(b == PASSES - 1),
                )
        for c in range(PICKS // P):
            result = ring.tile([P, PICKS], F32, name="result", bufs=4)
            nc.vector.tensor_tensor(result[:], scores[c][:], pair_tile[0][:, c, :], ALU.add)
            nc.sync.dma_start(out[c * P : (c + 1) * P, :], result[:])
